import numpy as np
import ml_dtypes


def mxq(x, axis, fmt="e4m3"):
    dtype, down = {"e4m3": (ml_dtypes.float8_e4m3fn, 7), "e5m2": (ml_dtypes.float8_e5m2, 14)}[fmt]
    v = np.moveaxis(np.asarray(x, np.float32).astype(ml_dtypes.bfloat16).astype(np.float64), axis, -1)
    blocks = v.reshape(v.shape[:-1] + (-1, 32))
    amax = np.abs(blocks).max(-1, keepdims=True)
    byte = np.maximum(np.where(amax > 0, np.frexp(amax)[1] - 1 + 127, 0) - down, 1)
    scale = np.exp2(byte - 127.0)
    codes = (blocks / scale).astype(np.float32).astype(dtype).astype(np.float64)
    return np.moveaxis((codes * scale).reshape(v.shape), -1, axis)


WIDE = False


def mx_kscale(k):
    if not WIDE:
        return np.ones(k)
    levels = np.array([10, -10, 5, -5, 0])
    if k % 512:
        return np.exp2(np.random.permutation(np.resize(levels, k // 32))).repeat(32)
    a = np.empty((k // 512, 16))
    for p in range(k // 512):
        a[p, :8] = np.random.permutation(np.resize(levels, 8))
        for g in range(8):
            far = levels[np.abs(levels - a[p, g]) >= 10]
            a[p, g + 8] = far[np.random.randint(len(far))]
    return np.exp2(a.ravel()).repeat(32)


def f64(x):
    return np.asarray(x).astype(np.float64)


def striped(idx):
    return np.tile(idx.reshape(-1, 16).T, (8, 1)).astype(np.uint16)


def unstriped(offs):
    return offs[:16].T.reshape(-1).astype(np.int64)


def striped8(idx):
    return np.concatenate([x.reshape(-1, 16).T for x in idx]).astype(np.uint16)


def runs(offs, k):
    lists = np.stack([offs[16 * r : 16 * r + 16].T.reshape(-1) for r in range(8)]).astype(np.int64)
    return lists[np.arange(k) % 512 // 64]


def pack_weight(w):
    k, n = w.shape
    w = f64(np.asarray(w, np.float32).astype(ml_dtypes.bfloat16)).reshape(k // 32, 32, n)
    amax = np.abs(w).max(1)
    byte = np.clip(np.where(amax > 0, np.frexp(amax)[1] - 1 + 127 - 7, 1), 1, 254)
    scaled = (w * np.exp2(127.0 - byte)[:, None, :]).reshape(k, n).astype(np.float32)
    words = np.ascontiguousarray(scaled.reshape(k // 512, 128, 4, n).transpose(0, 1, 3, 2)).astype(ml_dtypes.float8_e4m3fn).view(np.uint8)
    return words, np.ascontiguousarray(byte.astype(np.uint8).reshape(k // 512, 16, n))


def unpack_weight(words, scales):
    g, p, n, _ = words.shape
    vals = np.ascontiguousarray(words).view(ml_dtypes.float8_e4m3fn).astype(np.float64) * np.repeat(np.exp2(scales.astype(np.float64) - 127.0), 8, axis=1)[..., None]
    return vals.transpose(0, 1, 3, 2).reshape(g * 512, n)


K, T, S, N, H = 512, 2048, 512, 512, 512


def setup_inputs():
    n = np.random.standard_normal
    s = mx_kscale(K)[:, None]
    u = mx_kscale(S)
    packed_xT = pack_weight(n((K, T)) * s)
    return {
        "x_words": packed_xT[0],
        "x_scales": packed_xT[1],
        "wa": (n((K, H)) / np.sqrt(K) / s).astype(np.float32),
        "gt": (np.random.uniform(0.5, 1.5, (S, 1)) * u[:, None]).astype(np.float32),
        "w1": (n((S, N)) / np.sqrt(S) / u[:, None]).astype(np.float32),
        "offs": striped(np.random.permutation(T)[:S]),
        "fa": striped8(np.stack([np.random.permutation(H) for _ in range(8)])),
        "fb": striped8(np.stack([np.random.permutation(H) for _ in range(8)])),
    }


def reference(x_words, x_scales, wa, gt, w1, offs, fa, fb):
    xq = unpack_weight(x_words, x_scales)[:, unstriped(offs)]
    y = xq.T @ mxq(f64(wa), 0, "e4m3")
    a = y[np.arange(S)[:, None], runs(fa, S)]
    b = y[np.arange(S)[:, None], runs(fb, S)]
    z = f64(gt) * (np.maximum(np.minimum(y, a), np.minimum(np.maximum(y, a), b)))
    return mxq(f64(w1), 0, "e4m3").T @ mxq(z, 0, "e4m3")

@@ -1,0 +1,214 @@
+from contextlib import ExitStack
+
+import concourse.mybir as mybir
+
+K, T, S, N, H = 512, 2048, 512, 512, 512
+FLOPS = 2 * K * S * H + 2 * S * N * H
+
+F32 = mybir.dt.float32
+BF16 = mybir.dt.bfloat16
+I32 = mybir.dt.int32
+U32 = mybir.dt.uint32
+U16 = mybir.dt.uint16
+U8 = mybir.dt.uint8
+FP8X4 = mybir.dt.float8_e4m3fn_x4
+COPY = mybir.ActivationFunctionType.Copy
+MIN = mybir.AluOpType.min
+MAX = mybir.AluOpType.max
+MULT = mybir.AluOpType.mult
+
+P = 128
+PACK = 4
+HALF = H // 2
+CHUNKS = (256, 128, 128)
+WA_VECTOR_COLS = 160
+
+
+def tile_picked_featmed_none_p_kernel(tc, x_words, x_scales, wa, gt, w1, offs, fa, fb, out):
+    nc = tc.nc
+    with ExitStack() as ctx:
+        keep = ctx.enter_context(tc.tile_pool(name="keep", bufs=1))
+        psum = ctx.enter_context(tc.psum_pool(name="psum", bufs=8))
+
+        def sb(name, shape, dtype, tag=None):
+            return keep.tile(shape, dtype, name=name, tag=tag or name, align_bytes=64)
+
+        offs_sb = sb("offs_sb", [P, S // 16], U16)
+        fa_sb = sb("fa_sb", [P, H // 16], U16)
+        fb_sb = sb("fb_sb", [P, H // 16], U16)
+        x_table = sb("x_table", [P, T], U32)
+        s_table = sb("s_table", [P, T], U8)
+        gate = sb("gate", [P, PACK], F32)
+        wa_raw = [sb("wa_raw%d" % h, [P, PACK, HALF], F32) for h in range(2)]
+        w1_raw = sb("w1_raw", [P, PACK, N], F32)
+
+        nc.gpsimd.memset(s_table[:].bitcast(I32), 0)
+        nc.sync.dma_start(offs_sb[:], offs)
+        nc.sync.dma_start(x_table[:].bitcast(I32), x_words[0].rearrange("p n r -> p (n r)").bitcast(I32))
+        for q in range(4):
+            nc.sync.dma_start(s_table[32 * q : 32 * q + 4, :].bitcast(I32), x_scales[0, 4 * q : 4 * q + 4, :].bitcast(I32))
+        wa_rows = wa.rearrange("(p t) j -> p t j", t=PACK)
+        for h in range(2):
+            nc.sync.dma_start(wa_raw[h][:], wa_rows[:, :, h * HALF : (h + 1) * HALF])
+        nc.sync.dma_start(gate[:], gt.rearrange("(p t) o -> p (t o)", t=PACK))
+        nc.sync.dma_start(fa_sb[:], fa)
+        nc.sync.dma_start(fb_sb[:], fb)
+        nc.sync.dma_start(w1_raw[:], w1.rearrange("(p t) m -> p t m", t=PACK))
+
+        s_picked = sb("s_picked", [P, S], U8)
+        s_dealt = sb("s_dealt", [P, S], U8)
+        x_dealt = sb("x_dealt", [P, S], U32)
+        nc.vector.tensor_copy(s_picked[:], s_table[:].indirect(offs_sb[:]))
+        nc.vector.tensor_copy(x_dealt[:].rearrange("p (t m) -> p m t", t=PACK), x_table[:].indirect(offs_sb[:]))
+        nc.vector.tensor_copy(
+            s_dealt[:].rearrange("p (t m) -> p t m", t=PACK), s_picked[:].rearrange("p (m t) -> p t m", t=PACK)
+        )
+
+        def weave(engine, dst, src):
+            d = dst.rearrange("p (c i) t -> p c t i", i=4)
+            s = src.rearrange("p t (c i) -> p c t i", i=4)
+            if engine == "vector":
+                nc.vector.tensor_copy(d, s)
+            else:
+                nc.scalar.copy(d, s)
+
+        def quantize(codes, scales, woven):
+            nc.vector.quantize_mx(out=codes.bitcast(FP8X4), scales=scales, in_=woven.rearrange("p c t -> p (c t)"))
+
+        wa_woven = [sb("wa_woven%d" % h, [P, HALF, PACK], BF16) for h in range(2)]
+        wa_codes = [sb("wa_codes%d" % h, [P, HALF], U32) for h in range(2)]
+        wa_scales = [sb("wa_scales%d" % h, [P, HALF], U8) for h in range(2)]
+        weave("vector", wa_woven[0][:], wa_raw[0][:])
+        c = WA_VECTOR_COLS
+        weave("scalar", wa_woven[1][:, c:, :], wa_raw[1][:, :, c:])
+        quantize(wa_codes[0][:], wa_scales[0][:], wa_woven[0][:])
+        weave("vector", wa_woven[1][:, :c, :], wa_raw[1][:, :, :c])
+        quantize(wa_codes[1][:], wa_scales[1][:], wa_woven[1][:])
+
+        y = [sb("y%d" % t, [P, H], F32) for t in range(PACK)]
+        y_bf = sb("y_bf", [P, PACK, H], BF16)
+        banks = {}
+        for h in range(2):
+            for t in range(PACK):
+                bank = psum.tile([P, HALF], F32, name="bank")
+                banks[t, h] = bank
+                nc.tensor.matmul_mx(
+                    out=bank[:],
+                    lhsT=x_dealt[:, t * P : (t + 1) * P].bitcast(FP8X4),
+                    lhsT_scale=s_dealt[:, t * P : (t + 1) * P],
+                    rhs=wa_codes[h][:].bitcast(FP8X4),
+                    rhs_scale=wa_scales[h][:],
+                    start=True,
+                    stop=True,
+                )
+        for t in range(PACK):
+            for h in range(2):
+                dst = y[t][:, h * HALF : (h + 1) * HALF]
+                if (t, h) == (0, 1):
+                    nc.vector.tensor_scalar(dst, banks[t, h][:], gate[:, t : t + 1], None, MULT)
+                else:
+                    nc.scalar.activation(dst, banks[t, h][:], COPY, scale=gate[:, t : t + 1])
+        for h in range(2):
+            for t in range(PACK):
+                nc.scalar.copy(y_bf[:, t, h * HALF : (h + 1) * HALF], y[t][:, h * HALF : (h + 1) * HALF])
+
+        w1_woven = sb("w1_woven", [P, N, PACK], BF16)
+        w1_codes = sb("w1_codes", [P, N], U32)
+        w1_scales = sb("w1_scales", [P, N], U8)
+        for mt in range(PACK):
+            weave("scalar", w1_woven[:, mt * P : (mt + 1) * P, :], w1_raw[:, :, mt * P : (mt + 1) * P])
+
+        out_rows = out.rearrange("(mt p) j -> p mt j", p=P)
+        starts = [sum(CHUNKS[:i]) for i in range(len(CHUNKS))]
+        tiles = {}
+        slot = {("lo", 1): "woven0", ("mid", 2): "woven1"}
+
+        def work(kind, i):
+            if (kind, i) not in tiles:
+                w = CHUNKS[i]
+                shape, dtype = {
+                    "woven": ([P, w, PACK], BF16),
+                    "codes": ([P, w], U32),
+                    "scales": ([P, w], U8),
+                    "res": ([P, PACK, w], F32),
+                }.get(kind, ([P, PACK, w], BF16))
+                name = "%s%d" % (kind, i)
+                tag = kind if kind in ("a", "b") else slot.get((kind, i), name)
+                tiles[kind, i] = sb(name, shape, dtype, tag)
+            return tiles[kind, i]
+
+        def gather(i, which, t):
+            lst = fa_sb if which == "a" else fb_sb
+            cols = lst[:, starts[i] // 16 : (starts[i] + CHUNKS[i]) // 16]
+            nc.vector.tensor_copy(work(which, i)[:, t, :], y[t][:].indirect(cols))
+
+        def low_high(i):
+            own = y_bf[:, :, starts[i] : starts[i] + CHUNKS[i]]
+            nc.vector.tensor_tensor(work("lo", i)[:], own, work("a", i)[:], MIN)
+            nc.vector.tensor_tensor(work("hi", i)[:], own, work("a", i)[:], MAX)
+
+        def cap(i, ts):
+            nc.vector.tensor_tensor(work("mid", i)[:, ts, :], work("hi", i)[:, ts, :], work("b", i)[:, ts, :], MIN)
+
+        def median(i, ts):
+            nc.vector.tensor_tensor(work("z", i)[:, ts, :], work("lo", i)[:, ts, :], work("mid", i)[:, ts, :], MAX)
+
+        def mix(i):
+            w = CHUNKS[i]
+            last = i == len(CHUNKS) - 1
+            quantize(work("codes", i)[:], work("scales", i)[:], work("woven", i)[:])
+            for pair in range(2):
+                bank = psum.tile([P, 2, w], F32, name="bank")
+                for u in range(2):
+                    mt = 2 * pair + u
+                    nc.tensor.matmul_mx(
+                        out=bank[:, u, :],
+                        lhsT=w1_codes[:, mt * P : (mt + 1) * P].bitcast(FP8X4),
+                        lhsT_scale=w1_scales[:, mt * P : (mt + 1) * P],
+                        rhs=work("codes", i)[:].bitcast(FP8X4),
+                        rhs_scale=work("scales", i)[:],
+                        start=True,
+                        stop=True,
+                    )
+                dst = work("res", i)[:, 2 * pair : 2 * pair + 2, :]
+                if last and pair == 1:
+                    nc.vector.tensor_copy(dst, bank[:])
+                else:
+                    nc.scalar.copy(dst, bank[:])
+                nc.sync.dma_start(out_rows[:, 2 * pair : 2 * pair + 2, starts[i] : starts[i] + w], dst)
+
+        every = slice(0, PACK)
+        for t in range(PACK):
+            gather(0, "a", t)
+            gather(0, "b", t)
+        low_high(0)
+        quantize(w1_codes[:], w1_scales[:], w1_woven[:])
+        cap(0, every)
+        gather(1, "a", 0)
+        median(0, every)
+        weave("scalar", work("woven", 0)[:], work("z", 0)[:])
+        for t in range(1, PACK):
+            gather(1, "a", t)
+        for t in range(PACK):
+            gather(1, "b", t)
+        mix(0)
+        low_high(1)
+        gather(2, "a", 0)
+        cap(1, every)
+        gather(2, "a", 1)
+        median(1, every)
+        weave("scalar", work("woven", 1)[:], work("z", 1)[:])
+        gather(2, "a", 2)
+        gather(2, "a", 3)
+        gather(2, "b", 0)
+        low_high(2)
+        mix(1)
+        gather(2, "b", 1)
+        gather(2, "b", 2)
+        cap(2, slice(0, 2))
+        gather(2, "b", 3)
+        median(2, slice(0, 2))
+        cap(2, slice(2, 4))
+        median(2, slice(2, 4))
+        weave("vector", work("woven", 2)[:], work("z", 2)[:])
+        mix(2)

@@ -20,8 +20,7 @@ MULT = mybir.AluOpType.mult
 P = 128
 PACK = 4
 HALF = H // 2
-CHUNKS = (256, 128, 128)
-WA_VECTOR_COLS = 160
+QUARTER = H // 4
 
 
 def tile_picked_featmed_none_p_kernel(tc, x_words, x_scales, wa, gt, w1, offs, fa, fb, out):
@@ -39,30 +38,21 @@ def tile_picked_featmed_none_p_kernel(tc, x_words, x_scales, wa, gt, w1, offs, f
         x_table = sb("x_table", [P, T], U32)
         s_table = sb("s_table", [P, T], U8)
         gate = sb("gate", [P, PACK], F32)
-        wa_raw = [sb("wa_raw%d" % h, [P, PACK, HALF], F32) for h in range(2)]
-        w1_raw = sb("w1_raw", [P, PACK, N], F32)
 
-        nc.gpsimd.memset(s_table[:].bitcast(I32), 0)
-        nc.sync.dma_start(offs_sb[:], offs)
-        nc.sync.dma_start(x_table[:].bitcast(I32), x_words[0].rearrange("p n r -> p (n r)").bitcast(I32))
+        def load_half(name, w, h):
+            raw = sb("%s_raw%d" % (name, h), [P, PACK, HALF], F32, "raw%d" % h)
+            nc.sync.dma_start(raw[:], w.rearrange("(p t) j -> p t j", t=PACK)[:, :, h * HALF : (h + 1) * HALF])
+            return raw
+
+        nc.vector.memset(s_table[:].bitcast(I32), 0)
         for q in range(4):
-            nc.sync.dma_start(s_table[32 * q : 32 * q + 4, :].bitcast(I32), x_scales[0, 4 * q : 4 * q + 4, :].bitcast(I32))
-        wa_rows = wa.rearrange("(p t) j -> p t j", t=PACK)
-        for h in range(2):
-            nc.sync.dma_start(wa_raw[h][:], wa_rows[:, :, h * HALF : (h + 1) * HALF])
-        nc.sync.dma_start(gate[:], gt.rearrange("(p t) o -> p (t o)", t=PACK))
+            nc.scalar.dma_start(s_table[32 * q : 32 * q + 4, :].bitcast(I32), x_scales[0, 4 * q : 4 * q + 4, :].bitcast(I32))
+        nc.sync.dma_start(offs_sb[:], offs)
         nc.sync.dma_start(fa_sb[:], fa)
+        wa_raw = [load_half("wa", wa, h) for h in range(2)]
+        nc.sync.dma_start(x_table[:].bitcast(I32), x_words[0].rearrange("p n r -> p (n r)").bitcast(I32))
         nc.sync.dma_start(fb_sb[:], fb)
-        nc.sync.dma_start(w1_raw[:], w1.rearrange("(p t) m -> p t m", t=PACK))
-
-        s_picked = sb("s_picked", [P, S], U8)
-        s_dealt = sb("s_dealt", [P, S], U8)
-        x_dealt = sb("x_dealt", [P, S], U32)
-        nc.vector.tensor_copy(s_picked[:], s_table[:].indirect(offs_sb[:]))
-        nc.vector.tensor_copy(x_dealt[:].rearrange("p (t m) -> p m t", t=PACK), x_table[:].indirect(offs_sb[:]))
-        nc.vector.tensor_copy(
-            s_dealt[:].rearrange("p (t m) -> p t m", t=PACK), s_picked[:].rearrange("p (m t) -> p t m", t=PACK)
-        )
+        nc.gpsimd.dma_start(gate[:], gt.rearrange("(p t) o -> p (t o)", t=PACK))
 
         def weave(engine, dst, src):
             d = dst.rearrange("p (c i) t -> p c t i", i=4)
@@ -75,23 +65,28 @@ def tile_picked_featmed_none_p_kernel(tc, x_words, x_scales, wa, gt, w1, offs, f
         def quantize(codes, scales, woven):
             nc.vector.quantize_mx(out=codes.bitcast(FP8X4), scales=scales, in_=woven.rearrange("p c t -> p (c t)"))
 
+        s_picked = sb("s_picked", [P, S], U8)
+        s_dealt = sb("s_dealt", [P, S], U8)
+        x_dealt = sb("x_dealt", [P, S], U32)
+        nc.vector.tensor_copy(s_picked[:], s_table[:].indirect(offs_sb[:]))
+        nc.vector.tensor_copy(
+            s_dealt[:].rearrange("p (t m) -> p t m", t=PACK), s_picked[:].rearrange("p (m t) -> p t m", t=PACK)
+        )
+
         wa_woven = [sb("wa_woven%d" % h, [P, HALF, PACK], BF16) for h in range(2)]
         wa_codes = [sb("wa_codes%d" % h, [P, HALF], U32) for h in range(2)]
         wa_scales = [sb("wa_scales%d" % h, [P, HALF], U8) for h in range(2)]
-        weave("vector", wa_woven[0][:], wa_raw[0][:])
-        c = WA_VECTOR_COLS
-        weave("scalar", wa_woven[1][:, c:, :], wa_raw[1][:, :, c:])
-        quantize(wa_codes[0][:], wa_scales[0][:], wa_woven[0][:])
-        weave("vector", wa_woven[1][:, :c, :], wa_raw[1][:, :, :c])
-        quantize(wa_codes[1][:], wa_scales[1][:], wa_woven[1][:])
+        for h in range(2):
+            weave("scalar", wa_woven[h][:], wa_raw[h][:])
+            quantize(wa_codes[h][:], wa_scales[h][:], wa_woven[h][:])
+        w1_raw = [load_half("w1", w1, h) for h in range(2)]
+        nc.vector.tensor_copy(x_dealt[:].rearrange("p (t m) -> p m t", t=PACK), x_table[:].indirect(offs_sb[:]))
 
         y = [sb("y%d" % t, [P, H], F32) for t in range(PACK)]
         y_bf = sb("y_bf", [P, PACK, H], BF16)
-        banks = {}
-        for h in range(2):
-            for t in range(PACK):
+        for t in range(PACK):
+            for h in range(2):
                 bank = psum.tile([P, HALF], F32, name="bank")
-                banks[t, h] = bank
                 nc.tensor.matmul_mx(
                     out=bank[:],
                     lhsT=x_dealt[:, t * P : (t + 1) * P].bitcast(FP8X4),
@@ -101,13 +96,11 @@ def tile_picked_featmed_none_p_kernel(tc, x_words, x_scales, wa, gt, w1, offs, f
                     start=True,
                     stop=True,
                 )
-        for t in range(PACK):
-            for h in range(2):
                 dst = y[t][:, h * HALF : (h + 1) * HALF]
                 if (t, h) == (0, 1):
-                    nc.vector.tensor_scalar(dst, banks[t, h][:], gate[:, t : t + 1], None, MULT)
+                    nc.vector.tensor_scalar(dst, bank[:], gate[:, t : t + 1], None, MULT)
                 else:
-                    nc.scalar.activation(dst, banks[t, h][:], COPY, scale=gate[:, t : t + 1])
+                    nc.scalar.activation(dst, bank[:], COPY, scale=gate[:, t : t + 1])
         for h in range(2):
             for t in range(PACK):
                 nc.scalar.copy(y_bf[:, t, h * HALF : (h + 1) * HALF], y[t][:, h * HALF : (h + 1) * HALF])
@@ -115,100 +108,95 @@ def tile_picked_featmed_none_p_kernel(tc, x_words, x_scales, wa, gt, w1, offs, f
         w1_woven = sb("w1_woven", [P, N, PACK], BF16)
         w1_codes = sb("w1_codes", [P, N], U32)
         w1_scales = sb("w1_scales", [P, N], U8)
-        for mt in range(PACK):
-            weave("scalar", w1_woven[:, mt * P : (mt + 1) * P, :], w1_raw[:, :, mt * P : (mt + 1) * P])
+        for h in range(2):
+            weave("scalar", w1_woven[:, h * HALF : (h + 1) * HALF, :], w1_raw[h][:])
 
         out_rows = out.rearrange("(mt p) j -> p mt j", p=P)
-        starts = [sum(CHUNKS[:i]) for i in range(len(CHUNKS))]
-        tiles = {}
-        slot = {("lo", 1): "woven0", ("mid", 2): "woven1"}
 
-        def work(kind, i):
-            if (kind, i) not in tiles:
-                w = CHUNKS[i]
-                shape, dtype = {
-                    "woven": ([P, w, PACK], BF16),
-                    "codes": ([P, w], U32),
-                    "scales": ([P, w], U8),
-                    "res": ([P, PACK, w], F32),
-                }.get(kind, ([P, PACK, w], BF16))
-                name = "%s%d" % (kind, i)
-                tag = kind if kind in ("a", "b") else slot.get((kind, i), name)
-                tiles[kind, i] = sb(name, shape, dtype, tag)
-            return tiles[kind, i]
+        def planes(name, width, tag=None):
+            return sb(name, [P, PACK, width], BF16, tag)
 
-        def gather(i, which, t):
-            lst = fa_sb if which == "a" else fb_sb
-            cols = lst[:, starts[i] // 16 : (starts[i] + CHUNKS[i]) // 16]
-            nc.vector.tensor_copy(work(which, i)[:, t, :], y[t][:].indirect(cols))
+        def gather(dst, lists, j0, t):
+            width = dst.shape[2]
+            nc.vector.tensor_copy(dst[:, t, :], y[t][:].indirect(lists[:, j0 // 16 : (j0 + width) // 16]))
 
-        def low_high(i):
-            own = y_bf[:, :, starts[i] : starts[i] + CHUNKS[i]]
-            nc.vector.tensor_tensor(work("lo", i)[:], own, work("a", i)[:], MIN)
-            nc.vector.tensor_tensor(work("hi", i)[:], own, work("a", i)[:], MAX)
+        def pick(dst, u, v, op):
+            nc.vector.tensor_tensor(dst, u, v, op)
 
-        def cap(i, ts):
-            nc.vector.tensor_tensor(work("mid", i)[:, ts, :], work("hi", i)[:, ts, :], work("b", i)[:, ts, :], MIN)
-
-        def median(i, ts):
-            nc.vector.tensor_tensor(work("z", i)[:, ts, :], work("lo", i)[:, ts, :], work("mid", i)[:, ts, :], MAX)
-
-        def mix(i):
-            w = CHUNKS[i]
-            last = i == len(CHUNKS) - 1
-            quantize(work("codes", i)[:], work("scales", i)[:], work("woven", i)[:])
+        def mix(woven, j0, last):
+            width = woven.shape[1]
+            codes = sb("z_codes%d" % j0, [P, width], U32)
+            scales = sb("z_scales%d" % j0, [P, width], U8)
+            result = sb("result%d" % j0, [P, PACK, width], F32)
+            quantize(codes[:], scales[:], woven[:])
             for pair in range(2):
-                bank = psum.tile([P, 2, w], F32, name="bank")
+                bank = psum.tile([P, 2, width], F32, name="bank")
                 for u in range(2):
                     mt = 2 * pair + u
                     nc.tensor.matmul_mx(
                         out=bank[:, u, :],
                         lhsT=w1_codes[:, mt * P : (mt + 1) * P].bitcast(FP8X4),
                         lhsT_scale=w1_scales[:, mt * P : (mt + 1) * P],
-                        rhs=work("codes", i)[:].bitcast(FP8X4),
-                        rhs_scale=work("scales", i)[:],
+                        rhs=codes[:].bitcast(FP8X4),
+                        rhs_scale=scales[:],
                         start=True,
                         stop=True,
                     )
-                dst = work("res", i)[:, 2 * pair : 2 * pair + 2, :]
+                dst = result[:, 2 * pair : 2 * pair + 2, :]
                 if last and pair == 1:
                     nc.vector.tensor_copy(dst, bank[:])
                 else:
                     nc.scalar.copy(dst, bank[:])
-                nc.sync.dma_start(out_rows[:, 2 * pair : 2 * pair + 2, starts[i] : starts[i] + w], dst)
+                queue = nc.scalar if last and pair == 0 else nc.sync
+                queue.dma_start(out_rows[:, 2 * pair : 2 * pair + 2, j0 : j0 + width], dst)
 
-        every = slice(0, PACK)
+        a0 = planes("a0", HALF, "a")
+        b0 = planes("b0", HALF, "b")
         for t in range(PACK):
-            gather(0, "a", t)
-            gather(0, "b", t)
-        low_high(0)
+            gather(a0, fa_sb, 0, t)
+            gather(b0, fb_sb, 0, t)
+        lo0, hi0, mid0, z0 = [planes(n, HALF) for n in ("lo0", "hi0", "mid0", "z0")]
+        pick(hi0[:], y_bf[:, :, :HALF], a0[:], MAX)
+        pick(lo0[:], y_bf[:, :, :HALF], a0[:], MIN)
+        pick(mid0[:], hi0[:], b0[:], MIN)
+        a1 = planes("a1", HALF, "a")
+        gather(a1, fa_sb, HALF, 0)
+        pick(z0[:], lo0[:], mid0[:], MAX)
+        woven0 = sb("woven0", [P, HALF, PACK], BF16)
+        weave("scalar", woven0[:], z0[:])
         quantize(w1_codes[:], w1_scales[:], w1_woven[:])
-        cap(0, every)
-        gather(1, "a", 0)
-        median(0, every)
-        weave("scalar", work("woven", 0)[:], work("z", 0)[:])
         for t in range(1, PACK):
-            gather(1, "a", t)
-        for t in range(PACK):
-            gather(1, "b", t)
-        mix(0)
-        low_high(1)
-        gather(2, "a", 0)
-        cap(1, every)
-        gather(2, "a", 1)
-        median(1, every)
-        weave("scalar", work("woven", 1)[:], work("z", 1)[:])
-        gather(2, "a", 2)
-        gather(2, "a", 3)
-        gather(2, "b", 0)
-        low_high(2)
-        mix(1)
-        gather(2, "b", 1)
-        gather(2, "b", 2)
-        cap(2, slice(0, 2))
-        gather(2, "b", 3)
-        median(2, slice(0, 2))
-        cap(2, slice(2, 4))
-        median(2, slice(2, 4))
-        weave("vector", work("woven", 2)[:], work("z", 2)[:])
-        mix(2)
+            gather(a1, fa_sb, HALF, t)
+        mix(woven0, 0, False)
+        b1 = planes("b1", QUARTER, "b")
+        gather(b1, fb_sb, HALF, 0)
+        hi1 = planes("hi1", HALF, "woven0")
+        lo1 = planes("lo1", HALF)
+        pick(hi1[:], y_bf[:, :, HALF:], a1[:], MAX)
+        pick(lo1[:], y_bf[:, :, HALF:], a1[:], MIN)
+        for t in range(1, PACK):
+            gather(b1, fb_sb, HALF, t)
+        j2 = HALF + QUARTER
+        b2 = planes("b2", QUARTER, "a")
+        mid1, z1, mid2, z2 = [planes(n, QUARTER) for n in ("mid1", "z1", "mid2", "z2")]
+        gather(b2, fb_sb, j2, 0)
+        pick(mid1[:], hi1[:, :, :QUARTER], b1[:], MIN)
+        gather(b2, fb_sb, j2, 1)
+        pick(z1[:], lo1[:, :, :QUARTER], mid1[:], MAX)
+        woven1 = sb("woven1", [P, QUARTER, PACK], BF16)
+        weave("scalar", woven1[:], z1[:])
+        gather(b2, fb_sb, j2, 2)
+        pick(mid2[:, 0:2, :], hi1[:, 0:2, QUARTER:], b2[:, 0:2, :], MIN)
+        gather(b2, fb_sb, j2, 3)
+        pick(z2[:, 0:2, :], lo1[:, 0:2, QUARTER:], mid2[:, 0:2, :], MAX)
+        woven2 = sb("woven2", [P, QUARTER, PACK], BF16)
+        nc.scalar.copy(woven2[:, :, 0:2], z2[:, 0:2, :].rearrange("p t c -> p c t"))
+        pick(mid2[:, 2:4, :], hi1[:, 2:4, QUARTER:], b2[:, 2:4, :], MIN)
+        mix(woven1, HALF, False)
+        pick(
+            woven2[:, :, 2:4],
+            lo1[:, 2:4, QUARTER:].rearrange("p t c -> p c t"),
+            mid2[:, 2:4, :].rearrange("p t c -> p c t"),
+            MAX,
+        )
+        mix(woven2, j2, True)

@@ -19,6 +19,10 @@ MULT = mybir.AluOpType.mult
 
 P = 128
 PACK = 4
+QUADRANTS = 4
+LIST_ROWS = 16
+RUN = 4
+PSUM_BANKS = 8
 HALF = H // 2
 QUARTER = H // 4
 
@@ -27,14 +31,14 @@ def tile_picked_featmed_none_p_kernel(tc, x_words, x_scales, wa, gt, w1, offs, f
     nc = tc.nc
     with ExitStack() as ctx:
         keep = ctx.enter_context(tc.tile_pool(name="keep", bufs=1))
-        psum = ctx.enter_context(tc.psum_pool(name="psum", bufs=8))
+        psum = ctx.enter_context(tc.psum_pool(name="psum", bufs=PSUM_BANKS))
 
         def sb(name, shape, dtype, tag=None):
             return keep.tile(shape, dtype, name=name, tag=tag or name, align_bytes=64)
 
-        offs_sb = sb("offs_sb", [P, S // 16], U16)
-        fa_sb = sb("fa_sb", [P, H // 16], U16)
-        fb_sb = sb("fb_sb", [P, H // 16], U16)
+        offs_sb = sb("offs_sb", [P, S // LIST_ROWS], U16)
+        fa_sb = sb("fa_sb", [P, H // LIST_ROWS], U16)
+        fb_sb = sb("fb_sb", [P, H // LIST_ROWS], U16)
         x_table = sb("x_table", [P, T], U32)
         s_table = sb("s_table", [P, T], U8)
         gate = sb("gate", [P, PACK], F32)
@@ -45,22 +49,22 @@ def tile_picked_featmed_none_p_kernel(tc, x_words, x_scales, wa, gt, w1, offs, f
             return raw
 
         nc.vector.memset(s_table[:].bitcast(I32), 0)
-        for q in range(4):
-            nc.scalar.dma_start(s_table[32 * q : 32 * q + 4, :].bitcast(I32), x_scales[0, 4 * q : 4 * q + 4, :].bitcast(I32))
+        for q in range(QUADRANTS):
+            nc.scalar.dma_start(
+                s_table[32 * q : 32 * q + 4, :].bitcast(I32), x_scales[0, 4 * q : 4 * q + 4, :].bitcast(I32)
+            )
         nc.sync.dma_start(offs_sb[:], offs)
         nc.sync.dma_start(fa_sb[:], fa)
-        wa_raw = [load_half("wa", wa, h) for h in range(2)]
-        nc.sync.dma_start(x_table[:].bitcast(I32), x_words[0].rearrange("p n r -> p (n r)").bitcast(I32))
+        wa_raw = [load_half("wa", wa, 0)]
         nc.sync.dma_start(fb_sb[:], fb)
+        wa_raw.append(load_half("wa", wa, 1))
+        nc.sync.dma_start(x_table[:].bitcast(I32), x_words[0].rearrange("p n r -> p (n r)").bitcast(I32))
         nc.gpsimd.dma_start(gate[:], gt.rearrange("(p t) o -> p (t o)", t=PACK))
 
-        def weave(engine, dst, src):
-            d = dst.rearrange("p (c i) t -> p c t i", i=4)
-            s = src.rearrange("p t (c i) -> p c t i", i=4)
-            if engine == "vector":
-                nc.vector.tensor_copy(d, s)
-            else:
-                nc.scalar.copy(d, s)
+        def weave(dst, src):
+            nc.scalar.copy(
+                dst.rearrange("p (c i) t -> p c t i", i=RUN), src.rearrange("p t (c i) -> p c t i", i=RUN)
+            )
 
         def quantize(codes, scales, woven):
             nc.vector.quantize_mx(out=codes.bitcast(FP8X4), scales=scales, in_=woven.rearrange("p c t -> p (c t)"))
@@ -77,7 +81,7 @@ def tile_picked_featmed_none_p_kernel(tc, x_words, x_scales, wa, gt, w1, offs, f
         wa_codes = [sb("wa_codes%d" % h, [P, HALF], U32) for h in range(2)]
         wa_scales = [sb("wa_scales%d" % h, [P, HALF], U8) for h in range(2)]
         for h in range(2):
-            weave("scalar", wa_woven[h][:], wa_raw[h][:])
+            weave(wa_woven[h][:], wa_raw[h][:])
             quantize(wa_codes[h][:], wa_scales[h][:], wa_woven[h][:])
         w1_raw = [load_half("w1", w1, h) for h in range(2)]
         nc.vector.tensor_copy(x_dealt[:].rearrange("p (t m) -> p m t", t=PACK), x_table[:].indirect(offs_sb[:]))
@@ -96,11 +100,11 @@ def tile_picked_featmed_none_p_kernel(tc, x_words, x_scales, wa, gt, w1, offs, f
                     start=True,
                     stop=True,
                 )
-                dst = y[t][:, h * HALF : (h + 1) * HALF]
+                y_half = y[t][:, h * HALF : (h + 1) * HALF]
                 if (t, h) == (0, 1):
-                    nc.vector.tensor_scalar(dst, bank[:], gate[:, t : t + 1], None, MULT)
+                    nc.vector.tensor_scalar(y_half, bank[:], gate[:, t : t + 1], None, MULT)
                 else:
-                    nc.scalar.activation(dst, bank[:], COPY, scale=gate[:, t : t + 1])
+                    nc.scalar.activation(y_half, bank[:], COPY, scale=gate[:, t : t + 1])
         for h in range(2):
             for t in range(PACK):
                 nc.scalar.copy(y_bf[:, t, h * HALF : (h + 1) * HALF], y[t][:, h * HALF : (h + 1) * HALF])
@@ -109,7 +113,7 @@ def tile_picked_featmed_none_p_kernel(tc, x_words, x_scales, wa, gt, w1, offs, f
         w1_codes = sb("w1_codes", [P, N], U32)
         w1_scales = sb("w1_scales", [P, N], U8)
         for h in range(2):
-            weave("scalar", w1_woven[:, h * HALF : (h + 1) * HALF, :], w1_raw[h][:])
+            weave(w1_woven[:, h * HALF : (h + 1) * HALF, :], w1_raw[h][:])
 
         out_rows = out.rearrange("(mt p) j -> p mt j", p=P)
 
@@ -117,8 +121,8 @@ def tile_picked_featmed_none_p_kernel(tc, x_words, x_scales, wa, gt, w1, offs, f
             return sb(name, [P, PACK, width], BF16, tag)
 
         def gather(dst, lists, j0, t):
-            width = dst.shape[2]
-            nc.vector.tensor_copy(dst[:, t, :], y[t][:].indirect(lists[:, j0 // 16 : (j0 + width) // 16]))
+            entries = lists[:, j0 // LIST_ROWS : (j0 + dst.shape[2]) // LIST_ROWS]
+            nc.vector.tensor_copy(dst[:, t, :], y[t][:].indirect(entries))
 
         def pick(dst, u, v, op):
             nc.vector.tensor_tensor(dst, u, v, op)
@@ -142,20 +146,21 @@ def tile_picked_featmed_none_p_kernel(tc, x_words, x_scales, wa, gt, w1, offs, f
                         start=True,
                         stop=True,
                     )
-                dst = result[:, 2 * pair : 2 * pair + 2, :]
+                rows = result[:, 2 * pair : 2 * pair + 2, :]
                 if last and pair == 1:
-                    nc.vector.tensor_copy(dst, bank[:])
+                    nc.vector.tensor_copy(rows, bank[:])
                 else:
-                    nc.scalar.copy(dst, bank[:])
+                    nc.scalar.copy(rows, bank[:])
                 queue = nc.scalar if last and pair == 0 else nc.sync
-                queue.dma_start(out_rows[:, 2 * pair : 2 * pair + 2, j0 : j0 + width], dst)
+                queue.dma_start(out_rows[:, 2 * pair : 2 * pair + 2, j0 : j0 + width], rows)
+
 
         a0 = planes("a0", HALF, "a")
         b0 = planes("b0", HALF, "b")
         for t in range(PACK):
             gather(a0, fa_sb, 0, t)
             gather(b0, fb_sb, 0, t)
-        lo0, hi0, mid0, z0 = [planes(n, HALF) for n in ("lo0", "hi0", "mid0", "z0")]
+        lo0, hi0, mid0, z0 = [planes(name, HALF) for name in ("lo0", "hi0", "mid0", "z0")]
         pick(hi0[:], y_bf[:, :, :HALF], a0[:], MAX)
         pick(lo0[:], y_bf[:, :, :HALF], a0[:], MIN)
         pick(mid0[:], hi0[:], b0[:], MIN)
@@ -163,11 +168,12 @@ def tile_picked_featmed_none_p_kernel(tc, x_words, x_scales, wa, gt, w1, offs, f
         gather(a1, fa_sb, HALF, 0)
         pick(z0[:], lo0[:], mid0[:], MAX)
         woven0 = sb("woven0", [P, HALF, PACK], BF16)
-        weave("scalar", woven0[:], z0[:])
+        weave(woven0[:], z0[:])
         quantize(w1_codes[:], w1_scales[:], w1_woven[:])
         for t in range(1, PACK):
             gather(a1, fa_sb, HALF, t)
         mix(woven0, 0, False)
+
         b1 = planes("b1", QUARTER, "b")
         gather(b1, fb_sb, HALF, 0)
         hi1 = planes("hi1", HALF, "woven0")
@@ -176,27 +182,29 @@ def tile_picked_featmed_none_p_kernel(tc, x_words, x_scales, wa, gt, w1, offs, f
         pick(lo1[:], y_bf[:, :, HALF:], a1[:], MIN)
         for t in range(1, PACK):
             gather(b1, fb_sb, HALF, t)
-        j2 = HALF + QUARTER
+        last_j0 = HALF + QUARTER
         b2 = planes("b2", QUARTER, "a")
-        mid1, z1, mid2, z2 = [planes(n, QUARTER) for n in ("mid1", "z1", "mid2", "z2")]
-        gather(b2, fb_sb, j2, 0)
+        mid1, z1, mid2, z2 = [planes(name, QUARTER) for name in ("mid1", "z1", "mid2", "z2")]
+        gather(b2, fb_sb, last_j0, 0)
         pick(mid1[:], hi1[:, :, :QUARTER], b1[:], MIN)
-        gather(b2, fb_sb, j2, 1)
+        gather(b2, fb_sb, last_j0, 1)
         pick(z1[:], lo1[:, :, :QUARTER], mid1[:], MAX)
         woven1 = sb("woven1", [P, QUARTER, PACK], BF16)
-        weave("scalar", woven1[:], z1[:])
-        gather(b2, fb_sb, j2, 2)
-        pick(mid2[:, 0:2, :], hi1[:, 0:2, QUARTER:], b2[:, 0:2, :], MIN)
-        gather(b2, fb_sb, j2, 3)
-        pick(z2[:, 0:2, :], lo1[:, 0:2, QUARTER:], mid2[:, 0:2, :], MAX)
+        weave(woven1[:], z1[:])
+
+        early, late = slice(0, 2), slice(2, 4)
+        gather(b2, fb_sb, last_j0, 2)
+        pick(mid2[:, early, :], hi1[:, early, QUARTER:], b2[:, early, :], MIN)
+        gather(b2, fb_sb, last_j0, 3)
+        pick(z2[:, early, :], lo1[:, early, QUARTER:], mid2[:, early, :], MAX)
         woven2 = sb("woven2", [P, QUARTER, PACK], BF16)
-        nc.scalar.copy(woven2[:, :, 0:2], z2[:, 0:2, :].rearrange("p t c -> p c t"))
-        pick(mid2[:, 2:4, :], hi1[:, 2:4, QUARTER:], b2[:, 2:4, :], MIN)
+        nc.scalar.copy(woven2[:, :, early], z2[:, early, :].rearrange("p t c -> p c t"))
+        pick(mid2[:, late, :], hi1[:, late, QUARTER:], b2[:, late, :], MIN)
         mix(woven1, HALF, False)
         pick(
-            woven2[:, :, 2:4],
-            lo1[:, 2:4, QUARTER:].rearrange("p t c -> p c t"),
-            mid2[:, 2:4, :].rearrange("p t c -> p c t"),
+            woven2[:, :, late],
+            lo1[:, late, QUARTER:].rearrange("p t c -> p c t"),
+            mid2[:, late, :].rearrange("p t c -> p c t"),
             MAX,
         )
-        mix(woven2, j2, True)
+        mix(woven2, last_j0, True)

from contextlib import ExitStack

import concourse.mybir as mybir

K, T, S, N, H = 512, 2048, 512, 512, 512
FLOPS = 2 * K * S * H + 2 * S * N * H

F32 = mybir.dt.float32
BF16 = mybir.dt.bfloat16
I32 = mybir.dt.int32
U32 = mybir.dt.uint32
U16 = mybir.dt.uint16
U8 = mybir.dt.uint8
FP8X4 = mybir.dt.float8_e4m3fn_x4
COPY = mybir.ActivationFunctionType.Copy
MIN = mybir.AluOpType.min
MAX = mybir.AluOpType.max
MULT = mybir.AluOpType.mult

P = 128
PACK = 4
QUADRANTS = 4
LIST_ROWS = 16
RUN = 4
PSUM_BANKS = 8
HALF = H // 2
QUARTER = H // 4


def tile_picked_featmed_none_p_kernel(tc, x_words, x_scales, wa, gt, w1, offs, fa, fb, out):
    nc = tc.nc
    with ExitStack() as ctx:
        keep = ctx.enter_context(tc.tile_pool(name="keep", bufs=1))
        psum = ctx.enter_context(tc.psum_pool(name="psum", bufs=PSUM_BANKS))

        def sb(name, shape, dtype, tag=None):
            return keep.tile(shape, dtype, name=name, tag=tag or name, align_bytes=64)

        offs_sb = sb("offs_sb", [P, S // LIST_ROWS], U16)
        fa_sb = sb("fa_sb", [P, H // LIST_ROWS], U16)
        fb_sb = sb("fb_sb", [P, H // LIST_ROWS], U16)
        x_table = sb("x_table", [P, T], U32)
        s_table = sb("s_table", [P, T], U8)
        gate = sb("gate", [P, PACK], F32)

        def load_half(name, w, h):
            raw = sb("%s_raw%d" % (name, h), [P, PACK, HALF], F32, "raw%d" % h)
            nc.sync.dma_start(raw[:], w.rearrange("(p t) j -> p t j", t=PACK)[:, :, h * HALF : (h + 1) * HALF])
            return raw

        nc.vector.memset(s_table[:].bitcast(I32), 0)
        for q in range(QUADRANTS):
            nc.scalar.dma_start(
                s_table[32 * q : 32 * q + 4, :].bitcast(I32), x_scales[0, 4 * q : 4 * q + 4, :].bitcast(I32)
            )
        nc.sync.dma_start(offs_sb[:], offs)
        nc.sync.dma_start(fa_sb[:], fa)
        wa_raw = [load_half("wa", wa, 0)]
        nc.sync.dma_start(fb_sb[:], fb)
        wa_raw.append(load_half("wa", wa, 1))
        nc.sync.dma_start(x_table[:].bitcast(I32), x_words[0].rearrange("p n r -> p (n r)").bitcast(I32))
        nc.gpsimd.dma_start(gate[:], gt.rearrange("(p t) o -> p (t o)", t=PACK))

        def weave(dst, src):
            nc.scalar.copy(
                dst.rearrange("p (c i) t -> p c t i", i=RUN), src.rearrange("p t (c i) -> p c t i", i=RUN)
            )

        def quantize(codes, scales, woven):
            nc.vector.quantize_mx(out=codes.bitcast(FP8X4), scales=scales, in_=woven.rearrange("p c t -> p (c t)"))

        s_picked = sb("s_picked", [P, S], U8)
        s_dealt = sb("s_dealt", [P, S], U8)
        x_dealt = sb("x_dealt", [P, S], U32)
        nc.vector.tensor_copy(s_picked[:], s_table[:].indirect(offs_sb[:]))
        nc.vector.tensor_copy(
            s_dealt[:].rearrange("p (t m) -> p t m", t=PACK), s_picked[:].rearrange("p (m t) -> p t m", t=PACK)
        )

        wa_woven = [sb("wa_woven%d" % h, [P, HALF, PACK], BF16) for h in range(2)]
        wa_codes = [sb("wa_codes%d" % h, [P, HALF], U32) for h in range(2)]
        wa_scales = [sb("wa_scales%d" % h, [P, HALF], U8) for h in range(2)]
        for h in range(2):
            weave(wa_woven[h][:], wa_raw[h][:])
            quantize(wa_codes[h][:], wa_scales[h][:], wa_woven[h][:])
        w1_raw = [load_half("w1", w1, h) for h in range(2)]
        nc.vector.tensor_copy(x_dealt[:].rearrange("p (t m) -> p m t", t=PACK), x_table[:].indirect(offs_sb[:]))

        y = [sb("y%d" % t, [P, H], F32) for t in range(PACK)]
        y_bf = sb("y_bf", [P, PACK, H], BF16)
        for t in range(PACK):
            for h in range(2):
                bank = psum.tile([P, HALF], F32, name="bank")
                nc.tensor.matmul_mx(
                    out=bank[:],
                    lhsT=x_dealt[:, t * P : (t + 1) * P].bitcast(FP8X4),
                    lhsT_scale=s_dealt[:, t * P : (t + 1) * P],
                    rhs=wa_codes[h][:].bitcast(FP8X4),
                    rhs_scale=wa_scales[h][:],
                    start=True,
                    stop=True,
                )
                y_half = y[t][:, h * HALF : (h + 1) * HALF]
                if (t, h) == (0, 1):
                    nc.vector.tensor_scalar(y_half, bank[:], gate[:, t : t + 1], None, MULT)
                else:
                    nc.scalar.activation(y_half, bank[:], COPY, scale=gate[:, t : t + 1])
        for h in range(2):
            for t in range(PACK):
                nc.scalar.copy(y_bf[:, t, h * HALF : (h + 1) * HALF], y[t][:, h * HALF : (h + 1) * HALF])

        w1_woven = sb("w1_woven", [P, N, PACK], BF16)
        w1_codes = sb("w1_codes", [P, N], U32)
        w1_scales = sb("w1_scales", [P, N], U8)
        for h in range(2):
            weave(w1_woven[:, h * HALF : (h + 1) * HALF, :], w1_raw[h][:])

        out_rows = out.rearrange("(mt p) j -> p mt j", p=P)

        def planes(name, width, tag=None):
            return sb(name, [P, PACK, width], BF16, tag)

        def gather(dst, lists, j0, t):
            entries = lists[:, j0 // LIST_ROWS : (j0 + dst.shape[2]) // LIST_ROWS]
            nc.vector.tensor_copy(dst[:, t, :], y[t][:].indirect(entries))

        def pick(dst, u, v, op):
            nc.vector.tensor_tensor(dst, u, v, op)

        def mix(woven, j0, last):
            width = woven.shape[1]
            codes = sb("z_codes%d" % j0, [P, width], U32)
            scales = sb("z_scales%d" % j0, [P, width], U8)
            result = sb("result%d" % j0, [P, PACK, width], F32)
            quantize(codes[:], scales[:], woven[:])
            for pair in range(2):
                bank = psum.tile([P, 2, width], F32, name="bank")
                for u in range(2):
                    mt = 2 * pair + u
                    nc.tensor.matmul_mx(
                        out=bank[:, u, :],
                        lhsT=w1_codes[:, mt * P : (mt + 1) * P].bitcast(FP8X4),
                        lhsT_scale=w1_scales[:, mt * P : (mt + 1) * P],
                        rhs=codes[:].bitcast(FP8X4),
                        rhs_scale=scales[:],
                        start=True,
                        stop=True,
                    )
                rows = result[:, 2 * pair : 2 * pair + 2, :]
                if last and pair == 1:
                    nc.vector.tensor_copy(rows, bank[:])
                else:
                    nc.scalar.copy(rows, bank[:])
                queue = nc.scalar if last and pair == 0 else nc.sync
                queue.dma_start(out_rows[:, 2 * pair : 2 * pair + 2, j0 : j0 + width], rows)


        a0 = planes("a0", HALF, "a")
        b0 = planes("b0", HALF, "b")
        for t in range(PACK):
            gather(a0, fa_sb, 0, t)
            gather(b0, fb_sb, 0, t)
        lo0, hi0, mid0, z0 = [planes(name, HALF) for name in ("lo0", "hi0", "mid0", "z0")]
        pick(hi0[:], y_bf[:, :, :HALF], a0[:], MAX)
        pick(lo0[:], y_bf[:, :, :HALF], a0[:], MIN)
        pick(mid0[:], hi0[:], b0[:], MIN)
        a1 = planes("a1", HALF, "a")
        gather(a1, fa_sb, HALF, 0)
        pick(z0[:], lo0[:], mid0[:], MAX)
        woven0 = sb("woven0", [P, HALF, PACK], BF16)
        weave(woven0[:], z0[:])
        quantize(w1_codes[:], w1_scales[:], w1_woven[:])
        for t in range(1, PACK):
            gather(a1, fa_sb, HALF, t)
        mix(woven0, 0, False)

        b1 = planes("b1", QUARTER, "b")
        gather(b1, fb_sb, HALF, 0)
        hi1 = planes("hi1", HALF, "woven0")
        lo1 = planes("lo1", HALF)
        pick(hi1[:], y_bf[:, :, HALF:], a1[:], MAX)
        pick(lo1[:], y_bf[:, :, HALF:], a1[:], MIN)
        for t in range(1, PACK):
            gather(b1, fb_sb, HALF, t)
        last_j0 = HALF + QUARTER
        b2 = planes("b2", QUARTER, "a")
        mid1, z1, mid2, z2 = [planes(name, QUARTER) for name in ("mid1", "z1", "mid2", "z2")]
        gather(b2, fb_sb, last_j0, 0)
        pick(mid1[:], hi1[:, :, :QUARTER], b1[:], MIN)
        gather(b2, fb_sb, last_j0, 1)
        pick(z1[:], lo1[:, :, :QUARTER], mid1[:], MAX)
        woven1 = sb("woven1", [P, QUARTER, PACK], BF16)
        weave(woven1[:], z1[:])

        early, late = slice(0, 2), slice(2, 4)
        gather(b2, fb_sb, last_j0, 2)
        pick(mid2[:, early, :], hi1[:, early, QUARTER:], b2[:, early, :], MIN)
        gather(b2, fb_sb, last_j0, 3)
        pick(z2[:, early, :], lo1[:, early, QUARTER:], mid2[:, early, :], MAX)
        woven2 = sb("woven2", [P, QUARTER, PACK], BF16)
        nc.scalar.copy(woven2[:, :, early], z2[:, early, :].rearrange("p t c -> p c t"))
        pick(mid2[:, late, :], hi1[:, late, QUARTER:], b2[:, late, :], MIN)
        mix(woven1, HALF, False)
        pick(
            woven2[:, :, late],
            lo1[:, late, QUARTER:].rearrange("p t c -> p c t"),
            mid2[:, late, :].rearrange("p t c -> p c t"),
            MAX,
        )
        mix(woven2, last_j0, True)
